import numpy as np
import ml_dtypes


def mxq(x, axis, fmt="e4m3"):
    dtype, down = {"e4m3": (ml_dtypes.float8_e4m3fn, 7), "e5m2": (ml_dtypes.float8_e5m2, 14)}[fmt]
    v = np.moveaxis(np.asarray(x, np.float32).astype(ml_dtypes.bfloat16).astype(np.float64), axis, -1)
    blocks = v.reshape(v.shape[:-1] + (-1, 32))
    amax = np.abs(blocks).max(-1, keepdims=True)
    byte = np.maximum(np.where(amax > 0, np.frexp(amax)[1] - 1 + 127, 0) - down, 1)
    scale = np.exp2(byte - 127.0)
    codes = (blocks / scale).astype(np.float32).astype(dtype).astype(np.float64)
    return np.moveaxis((codes * scale).reshape(v.shape), -1, axis)


WIDE = False


def mx_kscale(k):
    if not WIDE:
        return np.ones(k)
    levels = np.array([10, -10, 5, -5, 0])
    if k % 512:
        return np.exp2(np.random.permutation(np.resize(levels, k // 32))).repeat(32)
    a = np.empty((k // 512, 16))
    for p in range(k // 512):
        a[p, :8] = np.random.permutation(np.resize(levels, 8))
        for g in range(8):
            far = levels[np.abs(levels - a[p, g]) >= 10]
            a[p, g + 8] = far[np.random.randint(len(far))]
    return np.exp2(a.ravel()).repeat(32)


def f64(x):
    return np.asarray(x).astype(np.float64)


def striped(idx):
    return np.tile(idx.reshape(-1, 16).T, (8, 1)).astype(np.uint16)


def unstriped(offs):
    return offs[:16].T.reshape(-1).astype(np.int64)


E2M1 = np.array([0.0, 0.5, 1.0, 1.5, 2.0, 3.0, 4.0, 6.0, -0.0, -0.5, -1.0, -1.5, -2.0, -3.0, -4.0, -6.0])


def pack_weight(w, fmt):
    k, n = w.shape
    w = f64(np.asarray(w, np.float32).astype(ml_dtypes.bfloat16)).reshape(k // 32, 32, n)
    amax = np.abs(w).max(1)
    if fmt == "e4m3":
        byte = np.frexp(amax)[1] - 1 + 127 - 7
    else:
        mant, ex = np.frexp(amax / 6.0)
        byte = np.where(mant > 0.5, ex, ex - 1) + 127
    byte = np.clip(np.where(amax > 0, byte, 1), 1, 254)
    scaled = (w * np.exp2(127.0 - byte)[:, None, :]).reshape(k, n).astype(np.float32)
    by_word = np.ascontiguousarray(scaled.reshape(k // 512, 128, 4, n).transpose(0, 1, 3, 2))
    if fmt == "e4m3":
        words = by_word.astype(ml_dtypes.float8_e4m3fn).view(np.uint8)
    else:
        c = by_word.astype(ml_dtypes.float4_e2m1fn).view(np.uint8) & 0xF
        words = (c[..., 0::2] | (c[..., 1::2] << 4)).reshape(k // 512, 128, 2 * n)
    return np.ascontiguousarray(words), np.ascontiguousarray(byte.astype(np.uint8).reshape(k // 512, 16, n))


def unpack_weight(words, scales, fmt):
    g, _, n = scales.shape
    words = np.ascontiguousarray(words).reshape(g, 128, n, -1)
    if fmt == "e4m3":
        vals = words.view(ml_dtypes.float8_e4m3fn).astype(np.float64)
    else:
        nib = np.empty((g, 128, n, 4), np.uint8)
        nib[..., 0::2] = words & 0xF
        nib[..., 1::2] = words >> 4
        vals = E2M1[nib]
    vals = vals * np.repeat(np.exp2(scales.astype(np.float64) - 127.0), 8, axis=1)[..., None]
    return vals.transpose(0, 1, 3, 2).reshape(g * 512, n)


def gelu(v):
    return 0.5 * v * (1.0 + np.tanh(np.sqrt(2.0 / np.pi) * (v + 0.044715 * v**3)))


def twice(P):
    return np.random.permutation(np.repeat(np.arange(P), 2))


K, H, T, S, P = 1536, 1024, 4096, 1024, 512


def setup_inputs():
    n = np.random.standard_normal
    s = mx_kscale(K)[:, None]
    u = mx_kscale(H)[:, None]
    d = {}
    d["tab_words"], d["tab_scales"] = pack_weight(n((K, T)) * s, "e4m3")
    d["offs"] = striped(np.random.permutation(T)[:S])
    perm = np.random.permutation(S)
    d["pos1"] = striped(perm[:P])
    d["pos2"] = striped(perm[P:2 * P])
    d["pos3"] = striped(twice(P))
    d["w1"] = (1.4 * n((K, H)) / s / K ** 0.5).astype(np.float32)
    d["b1"] = (0.5 * n(H)).astype(np.float32)
    d["gain"] = (np.exp(0.3 * n(H)) * u[:, 0]).astype(np.float32)
    d["w4_words"], d["w4_scales"] = pack_weight(1.1 * n((H, H)) / u / H ** 0.5, "e2m1")
    d["gs"] = (np.exp(0.3 * n(H)) / u[:, 0]).astype(np.float32)
    return d


def reference(tab_words, tab_scales, offs, pos1, pos2, pos3, w1, b1, gain, w4_words, w4_scales, gs):
    v = unpack_weight(tab_words, tab_scales, "e4m3")[:, unstriped(offs)]
    a = (mxq(f64(w1), 0, "e4m3").T @ v) + f64(b1)[:, None]
    h = f64(gain)[:, None] * (a / (1.0 + np.exp(-a)))
    z = h[:, unstriped(pos1)] - h[:, unstriped(pos2)]
    w4 = unpack_weight(w4_words, w4_scales, "e2m1")
    y = w4.T @ mxq(z, 0, "e4m3")
    up = y[:, unstriped(pos3)]
    return f64(gs)[:, None] * h - np.tanh(up)

@@ -1,0 +1,263 @@
+from contextlib import ExitStack
+
+import concourse.mybir as mybir
+
+K, H, T, S, M = 1536, 1024, 4096, 1024, 512
+FLOPS = 2 * K * H * S + 2 * H * H * M
+
+F32 = mybir.dt.float32
+BF16 = mybir.dt.bfloat16
+I32 = mybir.dt.int32
+U32 = mybir.dt.uint32
+U16 = mybir.dt.uint16
+U8 = mybir.dt.uint8
+FP8X4 = mybir.dt.float8_e4m3fn_x4
+FP4X4 = mybir.dt.float4_e2m1fn_x4
+ACT = mybir.ActivationFunctionType
+ALU = mybir.AluOpType
+
+P = 128
+PACK = 4
+KP = P * PACK
+BANK = 512
+PASS1 = K // KP
+PASS2 = H // KP
+TILES = H // P
+SPARE = 32
+
+
+def tile_list_linen_wear_scores_kernel(
+    tc, tab_words, tab_scales, offs, pos1, pos2, pos3, w1, b1, gain, w4_words, w4_scales, gs, out
+):
+    nc = tc.nc
+    with ExitStack() as ctx:
+        keep = ctx.enter_context(tc.tile_pool(name="keep", bufs=1))
+        ring = ctx.enter_context(tc.tile_pool(name="ring", bufs=2))
+        psum = ctx.enter_context(tc.psum_pool(name="psum", bufs=8))
+
+        offs_sb = keep.tile([P, S // 16], U16, name="offs_sb")
+        pos1_sb = keep.tile([P, M // 16], U16, name="pos1_sb")
+        pos2_sb = keep.tile([P, M // 16], U16, name="pos2_sb")
+        pos3_sb = keep.tile([P, S // 16], U16, name="pos3_sb")
+
+        tab_sc = keep.tile([P, T], U8, name="tab_sc", align_bytes=64)
+        w4_sc_raw = keep.tile([P, PASS2 * H], U8, name="w4_sc_raw", align_bytes=64)
+        zeros = keep.tile([P, SPARE], F32, name="zeros")
+        nc.vector.memset(tab_sc[:].bitcast(I32), 0)
+        nc.vector.memset(w4_sc_raw[:].bitcast(I32), 0)
+        nc.vector.memset(zeros[:], 0.0)
+        resp = [keep.tile([P, M + SPARE], F32, name="resp%d" % i) for i in range(TILES)]
+        for i in range(TILES):
+            nc.scalar.activation(resp[i][:, M:], zeros[:], ACT.Silu)
+
+        for q in range(4):
+            nc.gpsimd.dma_start(
+                out=tab_sc[32 * q : 32 * q + 4 * PASS1, :].bitcast(I32),
+                in_=tab_scales[:, 4 * q : 4 * q + 4, :].bitcast(I32),
+            )
+        for q in range(4):
+            nc.gpsimd.dma_start(
+                out=w4_sc_raw[32 * q : 32 * q + 4, :].bitcast(I32).rearrange("r (a n) -> r a n", a=PASS2),
+                in_=w4_scales[:, 4 * q : 4 * q + 4, :].bitcast(I32).rearrange("a r n -> r a n"),
+            )
+        b1_sb = keep.tile([P, PASS2, PACK], F32, name="b1_sb")
+        gain_sb = keep.tile([P, PASS2, PACK], F32, name="gain_sb")
+        gs_sb = keep.tile([P, PASS2, PACK], F32, name="gs_sb")
+        for dst, src in ((b1_sb, b1), (gain_sb, gain), (gs_sb, gs)):
+            nc.gpsimd.dma_start(out=dst[:], in_=src.rearrange("(b p t) -> p b t", b=PASS2, t=PACK))
+
+        tab_sb = [keep.tile([P, T], U32, name="tab%d" % a) for a in range(PASS1)]
+        w4_raw = keep.tile([P, PASS2 * 2 * H], U8, name="w4_raw")
+
+        def load_tab(a):
+            nc.sync.dma_start(
+                out=tab_sb[a][:].bitcast(I32),
+                in_=tab_words[a].rearrange("p t i -> p (t i)").bitcast(I32),
+            )
+
+        def load_w1(a, c0, width):
+            raw = ring.tile([P, PACK, width], F32, name="w1_raw", bufs=5)
+            nc.sync.dma_start(
+                out=raw[:],
+                in_=w1[a * KP : (a + 1) * KP, c0 : c0 + width].rearrange("(p j) c -> p j c", j=PACK),
+            )
+            return raw
+
+        nc.sync.dma_start(offs_sb[:], offs)
+        nc.sync.dma_start(
+            out=w4_raw[:].bitcast(I32).rearrange("p (a n) -> p a n", a=PASS2),
+            in_=w4_words.bitcast(I32).rearrange("a p n -> p a n"),
+        )
+        raw = {}
+        for a in range(PASS1):
+            load_tab(a)
+            if a < PASS1 - 1:
+                raw[(0, a)] = [load_w1(a, 0, KP)]
+            else:
+                raw[(0, a)] = [load_w1(a, 0, KP // 2), load_w1(a, KP // 2, KP // 2)]
+        nc.sync.dma_start(pos2_sb[:], pos2)
+        nc.sync.dma_start(pos1_sb[:], pos1)
+
+        w1_codes = {}
+        w1_sc = {}
+
+        def cast_w1(b, a):
+            grouped = ring.tile([P, PACK * KP], BF16, name="w1_bf", align_bytes=64)
+            view = grouped[:].rearrange("p (t m j) -> p m t j", t=PACK, j=PACK)
+            pieces = raw[(b, a)]
+            per = P // len(pieces)
+            for n, piece in enumerate(pieces):
+                src = piece[:].rearrange("p j (m t) -> p m t j", t=PACK)
+                dst = view[:, n * per : (n + 1) * per]
+                if n == 0:
+                    nc.scalar.copy(out=dst, in_=src)
+                else:
+                    nc.vector.tensor_copy(out=dst, in_=src)
+            return grouped
+
+        def quant_w1(b, a, grouped, parts):
+            codes = keep.tile([P, KP], U32, name="w1c%d%d" % (b, a), align_bytes=64)
+            sc = keep.tile([P, KP], U8, name="w1s%d%d" % (b, a), align_bytes=64)
+            w = KP // parts
+            for n in range(parts):
+                nc.vector.quantize_mx(
+                    out=codes[:, n * w : (n + 1) * w].bitcast(FP8X4),
+                    scales=sc[:, n * w : (n + 1) * w],
+                    in_=grouped[:, PACK * n * w : PACK * (n + 1) * w],
+                )
+            w1_codes[(b, a)] = codes
+            w1_sc[(b, a)] = sc
+
+        v_codes = [keep.tile([P, S], U32, name="v%d" % a, align_bytes=64) for a in range(PASS1)]
+        v_sc = keep.tile([P, S], U8, name="v_sc", align_bytes=64)
+
+        def gather_tab(a):
+            for half in range(S // BANK):
+                nc.vector.tensor_copy(
+                    v_codes[a][:, half * BANK : (half + 1) * BANK],
+                    tab_sb[a][:].indirect(offs_sb[:, half * (BANK // 16) : (half + 1) * (BANK // 16)]),
+                )
+
+        def mm1(acc, b, t, a, half):
+            cols = slice(half * BANK, (half + 1) * BANK)
+            rows = slice(t * P, (t + 1) * P)
+            nc.tensor.matmul_mx(
+                out=acc[:],
+                lhsT=w1_codes[(b, a)][:, rows].bitcast(FP8X4),
+                lhsT_scale=w1_sc[(b, a)][:, rows],
+                rhs=v_codes[a][:, cols].bitcast(FP8X4),
+                rhs_scale=v_sc[4 * a : P, cols],
+                start=(a == 0),
+                stop=(a == PASS1 - 1),
+            )
+
+        feat = [keep.tile([P, S], F32, name="feat%d" % i) for i in range(TILES)]
+
+        def silu(acc, b, t, half):
+            nc.scalar.activation(
+                feat[PACK * b + t][:, half * BANK : (half + 1) * BANK], acc[:], ACT.Silu, bias=b1_sb[:, b, t : t + 1]
+            )
+
+        w4_sb = keep.tile([P, PASS2 * 2 * H], U8, name="w4_sb", align_bytes=64)
+        w4_sc = keep.tile([P, PASS2 * H], U8, name="w4_sc", align_bytes=64)
+        accs = {}
+        for t in range(PACK):
+            for half in range(2):
+                accs[(t, half)] = psum.tile([P, BANK], F32, name="acc")
+        nc.vector.tensor_copy(v_sc[:], tab_sc[:].indirect(offs_sb[:]))
+        for a in range(PASS1):
+            gather_tab(a)
+            grouped = cast_w1(0, a)
+            quant_w1(0, a, grouped, PACK if a == PASS1 - 1 else 1)
+            for t in range(PACK):
+                for half in range(2):
+                    mm1(accs[(t, half)], 0, t, a, half)
+        for a in range(PASS1):
+            raw[(1, a)] = [load_w1(a, KP, KP)]
+        nc.sync.dma_start(pos3_sb[:], pos3)
+        for t in range(PACK):
+            for half in range(2):
+                silu(accs[(t, half)], 0, t, half)
+
+        for a in range(PASS2):
+            cols = slice(a * 2 * H, (a + 1) * 2 * H)
+            nc.vector.tensor_copy(
+                out=w4_sb[:, cols].rearrange("p (b t q e) -> p b t q e", b=PASS2, t=PACK, e=2),
+                in_=w4_raw[:, cols].rearrange("p (b q t e) -> p b t q e", b=PASS2, t=PACK, e=2),
+            )
+        nc.vector.tensor_copy(
+            out=w4_sc[:].rearrange("p (g t q) -> p g t q", t=PACK, q=P),
+            in_=w4_sc_raw[:].rearrange("p (g q t) -> p g t q", t=PACK, q=P),
+        )
+        both = keep.tile([P, PASS2, PACK], F32, name="both")
+        nc.vector.tensor_tensor(both[:], gs_sb[:], gain_sb[:], ALU.mult)
+
+        for a in range(PASS1):
+            grouped = cast_w1(1, a)
+            quant_w1(1, a, grouped, 1)
+        for t in range(PACK):
+            for half in range(2):
+                acc = psum.tile([P, BANK], F32, name="acc")
+                for a in range(PASS1):
+                    mm1(acc, 1, t, a, half)
+                silu(acc, 1, t, half)
+
+        planes = [keep.tile([P, PACK, M], BF16, name="zp%d" % b) for b in range(PASS2)]
+        z_codes = [keep.tile([P, M], U32, name="zc%d" % b, align_bytes=64) for b in range(PASS2)]
+        z_sc = [keep.tile([P, M], U8, name="zs%d" % b, align_bytes=64) for b in range(PASS2)]
+        second = {}
+
+        def pick_second(i):
+            second[i] = ring.tile([P, M], F32, name="second", bufs=3)
+            nc.vector.tensor_copy(second[i][:], feat[i][:].indirect(pos2_sb[:]))
+
+        def difference(i):
+            b, t = divmod(i, PACK)
+            diff = ring.tile([P, M], F32, name="diff", bufs=3)
+            nc.vector.tensor_tensor(diff[:], feat[i][:].indirect(pos1_sb[:]), second[i][:], ALU.subtract)
+            nc.scalar.activation(planes[b][:, t, :], diff[:], ACT.Copy, scale=gain_sb[:, b, t : t + 1])
+
+        def quant_z(b):
+            woven = ring.tile([P, M * PACK], BF16, name="woven", align_bytes=64)
+            dst = woven[:].rearrange("p (c i t) -> p c t i", i=4, t=PACK)
+            src = planes[b][:].rearrange("p t (c i) -> p c t i", i=4)
+            if b == 0:
+                nc.scalar.copy(out=dst, in_=src)
+            else:
+                nc.vector.tensor_copy(out=dst, in_=src)
+            nc.vector.quantize_mx(out=z_codes[b][:].bitcast(FP8X4), scales=z_sc[b][:], in_=woven[:])
+
+        pick_second(0)
+        for i in range(TILES):
+            if i + 1 < TILES:
+                pick_second(i + 1)
+            difference(i)
+            if i % PACK == PACK - 1:
+                quant_z(i // PACK)
+
+        out_rows = out.rearrange("(b p t) j -> b t p j", b=PASS2, t=PACK)
+        for i in range(TILES):
+            b, t = divmod(i, PACK)
+            acc = psum.tile([P, BANK], F32, name="acc")
+            for a in range(PASS2):
+                nc.tensor.matmul_mx(
+                    out=acc[:],
+                    lhsT=w4_sb[:, a * 2 * H + i * 2 * P : a * 2 * H + (i + 1) * 2 * P].bitcast(FP4X4),
+                    lhsT_scale=w4_sc[:, a * H + i * P : a * H + (i + 1) * P],
+                    rhs=z_codes[a][:].bitcast(FP8X4),
+                    rhs_scale=z_sc[a][:],
+                    start=(a == 0),
+                    stop=(a == PASS2 - 1),
+                )
+            nc.scalar.activation(resp[i][:, :M], acc[:], ACT.Tanh, scale=-1.0)
+            nc.scalar.activation(feat[i][:], feat[i][:], ACT.Copy, scale=both[:, b, t : t + 1])
+            for half in range(S // BANK):
+                cols = slice(half * BANK, (half + 1) * BANK)
+                res = ring.tile([P, BANK], F32, name="res", bufs=4)
+                nc.vector.tensor_tensor(
+                    res[:],
+                    resp[i][:].indirect(pos3_sb[:, half * (BANK // 16) : (half + 1) * (BANK // 16)]),
+                    feat[i][:, cols],
+                    ALU.add,
+                )
+                nc.sync.dma_start(out=out_rows[b, t][:, cols], in_=res[:])

@@ -44,7 +44,7 @@ def tile_list_linen_wear_scores_kernel(
         w4_sc_raw = keep.tile([P, PASS2 * H], U8, name="w4_sc_raw", align_bytes=64)
         zeros = keep.tile([P, SPARE], F32, name="zeros")
         nc.vector.memset(tab_sc[:].bitcast(I32), 0)
-        nc.vector.memset(w4_sc_raw[:].bitcast(I32), 0)
+        nc.gpsimd.memset(w4_sc_raw[:].bitcast(I32), 0)
         nc.vector.memset(zeros[:], 0.0)
         resp = [keep.tile([P, M + SPARE], F32, name="resp%d" % i) for i in range(TILES)]
         for i in range(TILES):
@@ -55,16 +55,12 @@ def tile_list_linen_wear_scores_kernel(
                 out=tab_sc[32 * q : 32 * q + 4 * PASS1, :].bitcast(I32),
                 in_=tab_scales[:, 4 * q : 4 * q + 4, :].bitcast(I32),
             )
-        for q in range(4):
-            nc.gpsimd.dma_start(
-                out=w4_sc_raw[32 * q : 32 * q + 4, :].bitcast(I32).rearrange("r (a n) -> r a n", a=PASS2),
-                in_=w4_scales[:, 4 * q : 4 * q + 4, :].bitcast(I32).rearrange("a r n -> r a n"),
-            )
-        b1_sb = keep.tile([P, PASS2, PACK], F32, name="b1_sb")
+        b1_sb = keep.tile([P, PASS2, PACK], F32, name="b1_sb", align_bytes=64)
         gain_sb = keep.tile([P, PASS2, PACK], F32, name="gain_sb")
         gs_sb = keep.tile([P, PASS2, PACK], F32, name="gs_sb")
-        for dst, src in ((b1_sb, b1), (gain_sb, gain), (gs_sb, gs)):
-            nc.gpsimd.dma_start(out=dst[:], in_=src.rearrange("(b p t) -> p b t", b=PASS2, t=PACK))
+
+        def load_vec(dst, src):
+            nc.sync.dma_start(out=dst[:], in_=src.rearrange("(b p t) -> p b t", b=PASS2, t=PACK))
 
         tab_sb = [keep.tile([P, T], U32, name="tab%d" % a) for a in range(PASS1)]
         w4_raw = keep.tile([P, PASS2 * 2 * H], U8, name="w4_raw")
@@ -76,40 +72,55 @@ def tile_list_linen_wear_scores_kernel(
             )
 
         def load_w1(a, c0, width):
-            raw = ring.tile([P, PACK, width], F32, name="w1_raw", bufs=5)
+            if width < KP:
+                raw = ring.tile([P, PACK, width], F32, name="w1_half")
+            elif c0 and a == PASS1 - 1:
+                raw = keep.tile([P, PACK, width], F32, name="raw_last")
+            else:
+                raw = ring.tile([P, PACK, width], F32, name="w1_raw")
             nc.sync.dma_start(
                 out=raw[:],
                 in_=w1[a * KP : (a + 1) * KP, c0 : c0 + width].rearrange("(p j) c -> p j c", j=PACK),
             )
             return raw
 
-        nc.sync.dma_start(offs_sb[:], offs)
         nc.sync.dma_start(
             out=w4_raw[:].bitcast(I32).rearrange("p (a n) -> p a n", a=PASS2),
             in_=w4_words.bitcast(I32).rearrange("a p n -> p a n"),
         )
+        nc.sync.dma_start(offs_sb[:], offs)
         raw = {}
-        for a in range(PASS1):
-            load_tab(a)
-            if a < PASS1 - 1:
-                raw[(0, a)] = [load_w1(a, 0, KP)]
-            else:
-                raw[(0, a)] = [load_w1(a, 0, KP // 2), load_w1(a, KP // 2, KP // 2)]
+        raw[(0, 0)] = [load_w1(0, 0, KP)]
+        load_tab(0)
+        raw[(0, 1)] = [load_w1(1, 0, KP)]
+        for q in range(4):
+            nc.sync.dma_start(
+                out=w4_sc_raw[32 * q : 32 * q + 4, :].bitcast(I32).rearrange("r (a n) -> r a n", a=PASS2),
+                in_=w4_scales[:, 4 * q : 4 * q + 4, :].bitcast(I32).rearrange("a r n -> r a n"),
+            )
+        load_vec(b1_sb, b1)
+        load_tab(1)
         nc.sync.dma_start(pos2_sb[:], pos2)
+        load_tab(2)
+        raw[(0, 2)] = [load_w1(2, 0, KP // 2), load_w1(2, KP // 2, KP // 2)]
+        load_vec(gain_sb, gain)
         nc.sync.dma_start(pos1_sb[:], pos1)
 
         w1_codes = {}
         w1_sc = {}
 
         def cast_w1(b, a):
-            grouped = ring.tile([P, PACK * KP], BF16, name="w1_bf", align_bytes=64)
+            if b == 1 and a > 0:
+                grouped = keep.tile([P, PACK * KP], BF16, name="w1_late%d" % a, align_bytes=64)
+            else:
+                grouped = ring.tile([P, PACK * KP], BF16, name="w1_bf", align_bytes=64)
             view = grouped[:].rearrange("p (t m j) -> p m t j", t=PACK, j=PACK)
             pieces = raw[(b, a)]
-            per = P // len(pieces)
-            for n, piece in enumerate(pieces):
-                src = piece[:].rearrange("p j (m t) -> p m t j", t=PACK)
+            srcs = [piece[:].rearrange("p j (m t) -> p m t j", t=PACK) for piece in pieces]
+            per = P // len(srcs)
+            for n, src in enumerate(srcs):
                 dst = view[:, n * per : (n + 1) * per]
-                if n == 0:
+                if n == 0 and (b, a) != (1, 0):
                     nc.scalar.copy(out=dst, in_=src)
                 else:
                     nc.vector.tensor_copy(out=dst, in_=src)
@@ -160,24 +171,21 @@ def tile_list_linen_wear_scores_kernel(
 
         w4_sb = keep.tile([P, PASS2 * 2 * H], U8, name="w4_sb", align_bytes=64)
         w4_sc = keep.tile([P, PASS2 * H], U8, name="w4_sc", align_bytes=64)
-        accs = {}
-        for t in range(PACK):
-            for half in range(2):
-                accs[(t, half)] = psum.tile([P, BANK], F32, name="acc")
         nc.vector.tensor_copy(v_sc[:], tab_sc[:].indirect(offs_sb[:]))
         for a in range(PASS1):
             gather_tab(a)
             grouped = cast_w1(0, a)
             quant_w1(0, a, grouped, PACK if a == PASS1 - 1 else 1)
-            for t in range(PACK):
-                for half in range(2):
-                    mm1(accs[(t, half)], 0, t, a, half)
         for a in range(PASS1):
             raw[(1, a)] = [load_w1(a, KP, KP)]
+        load_vec(gs_sb, gs)
         nc.sync.dma_start(pos3_sb[:], pos3)
         for t in range(PACK):
             for half in range(2):
-                silu(accs[(t, half)], 0, t, half)
+                acc = psum.tile([P, BANK], F32, name="acc")
+                for a in range(PASS1):
+                    mm1(acc, 0, t, a, half)
+                silu(acc, 0, t, half)
 
         for a in range(PASS2):
             cols = slice(a * 2 * H, (a + 1) * 2 * H)
@@ -189,12 +197,10 @@ def tile_list_linen_wear_scores_kernel(
             out=w4_sc[:].rearrange("p (g t q) -> p g t q", t=PACK, q=P),
             in_=w4_sc_raw[:].rearrange("p (g q t) -> p g t q", t=PACK, q=P),
         )
-        both = keep.tile([P, PASS2, PACK], F32, name="both")
-        nc.vector.tensor_tensor(both[:], gs_sb[:], gain_sb[:], ALU.mult)
 
         for a in range(PASS1):
             grouped = cast_w1(1, a)
-            quant_w1(1, a, grouped, 1)
+            quant_w1(1, a, grouped, PACK if a == PASS1 - 1 else 1)
         for t in range(PACK):
             for half in range(2):
                 acc = psum.tile([P, BANK], F32, name="acc")
@@ -202,7 +208,10 @@ def tile_list_linen_wear_scores_kernel(
                     mm1(acc, 1, t, a, half)
                 silu(acc, 1, t, half)
 
-        planes = [keep.tile([P, PACK, M], BF16, name="zp%d" % b) for b in range(PASS2)]
+        late = keep.tile([P, 2 * M + TILES], F32, name="w1c12", align_bytes=64)
+        early = keep.tile([P, 2 * M], F32, name="raw_last")
+        planes = [x[:, : 2 * M].bitcast(BF16).rearrange("p (t m) -> p t m", t=PACK) for x in (early, late)]
+        both = late[:, 2 * M :]
         z_codes = [keep.tile([P, M], U32, name="zc%d" % b, align_bytes=64) for b in range(PASS2)]
         z_sc = [keep.tile([P, M], U8, name="zs%d" % b, align_bytes=64) for b in range(PASS2)]
         second = {}
@@ -213,19 +222,30 @@ def tile_list_linen_wear_scores_kernel(
 
         def difference(i):
             b, t = divmod(i, PACK)
-            diff = ring.tile([P, M], F32, name="diff", bufs=3)
+            if i in (PACK - 2, PACK - 1):
+                diff = keep.tile([P, M], F32, name="w1_late%d" % (i - 1), align_bytes=64)
+            elif i == TILES - 1:
+                diff = keep.tile([P, M], F32, name="b1_sb", align_bytes=64)
+            else:
+                diff = ring.tile([P, M], F32, name="diff", bufs=4)
             nc.vector.tensor_tensor(diff[:], feat[i][:].indirect(pos1_sb[:]), second[i][:], ALU.subtract)
-            nc.scalar.activation(planes[b][:, t, :], diff[:], ACT.Copy, scale=gain_sb[:, b, t : t + 1])
+            if i < TILES - 1:
+                nc.scalar.activation(planes[b][:, t, :], diff[:], ACT.Copy, scale=gain_sb[:, b, t : t + 1])
+            else:
+                nc.vector.tensor_scalar(planes[b][:, t, :], diff[:], gain_sb[:, b, t : t + 1], None, ALU.mult)
 
         def quant_z(b):
-            woven = ring.tile([P, M * PACK], BF16, name="woven", align_bytes=64)
-            dst = woven[:].rearrange("p (c i t) -> p c t i", i=4, t=PACK)
-            src = planes[b][:].rearrange("p t (c i) -> p c t i", i=4)
+            if b == 0:
+                woven = keep.tile([P, M * PACK], BF16, name="b1_sb", align_bytes=64)[:]
+            else:
+                woven = ring.tile([P, M * PACK], BF16, name="w1_bf", align_bytes=64)[:]
+            dst = woven.rearrange("p (c i t) -> p c t i", i=4, t=PACK)
+            src = planes[b].rearrange("p t (c i) -> p c t i", i=4)
             if b == 0:
                 nc.scalar.copy(out=dst, in_=src)
             else:
                 nc.vector.tensor_copy(out=dst, in_=src)
-            nc.vector.quantize_mx(out=z_codes[b][:].bitcast(FP8X4), scales=z_sc[b][:], in_=woven[:])
+            nc.vector.quantize_mx(out=z_codes[b][:].bitcast(FP8X4), scales=z_sc[b][:], in_=woven)
 
         pick_second(0)
         for i in range(TILES):
@@ -235,6 +255,9 @@ def tile_list_linen_wear_scores_kernel(
             if i % PACK == PACK - 1:
                 quant_z(i // PACK)
 
+        nc.vector.tensor_tensor(
+            both, gs_sb[:].rearrange("p b t -> p (b t)"), gain_sb[:].rearrange("p b t -> p (b t)"), ALU.mult
+        )
         out_rows = out.rearrange("(b p t) j -> b t p j", b=PASS2, t=PACK)
         for i in range(TILES):
             b, t = divmod(i, PACK)
@@ -250,14 +273,15 @@ def tile_list_linen_wear_scores_kernel(
                     stop=(a == PASS2 - 1),
                 )
             nc.scalar.activation(resp[i][:, :M], acc[:], ACT.Tanh, scale=-1.0)
-            nc.scalar.activation(feat[i][:], feat[i][:], ACT.Copy, scale=both[:, b, t : t + 1])
             for half in range(S // BANK):
                 cols = slice(half * BANK, (half + 1) * BANK)
+                own = ring.tile([P, BANK], F32, name="own", bufs=4)
+                nc.scalar.activation(own[:], feat[i][:, cols], ACT.Copy, scale=both[:, i : i + 1])
                 res = ring.tile([P, BANK], F32, name="res", bufs=4)
                 nc.vector.tensor_tensor(
                     res[:],
                     resp[i][:].indirect(pos3_sb[:, half * (BANK // 16) : (half + 1) * (BANK // 16)]),
-                    feat[i][:, cols],
+                    own[:],
                     ALU.add,
                 )
                 nc.sync.dma_start(out=out_rows[b, t][:, cols], in_=res[:])

@@ -24,6 +24,8 @@ PASS1 = K // KP
 PASS2 = H // KP
 TILES = H // P
 SPARE = 32
+WINDOWS = 4
+HALF = M // 2
 
 
 def tile_list_linen_wear_scores_kernel(
@@ -42,12 +44,12 @@ def tile_list_linen_wear_scores_kernel(
 
         tab_sc = keep.tile([P, T], U8, name="tab_sc", align_bytes=64)
         w4_sc_raw = keep.tile([P, PASS2 * H], U8, name="w4_sc_raw", align_bytes=64)
-        zeros = keep.tile([P, SPARE], F32, name="zeros")
+        zeros = keep.tile([P, S + SPARE - M], F32, name="zeros")
         nc.vector.memset(tab_sc[:].bitcast(I32), 0)
         nc.gpsimd.memset(w4_sc_raw[:].bitcast(I32), 0)
         nc.vector.memset(zeros[:], 0.0)
-        resp = [keep.tile([P, M + SPARE], F32, name="resp%d" % i) for i in range(TILES)]
-        for i in range(TILES):
+        resp = [keep.tile([P, S + SPARE], F32, name="resp%d" % i) for i in range(WINDOWS)]
+        for i in range(WINDOWS):
             nc.scalar.activation(resp[i][:, M:], zeros[:], ACT.Silu)
 
         for q in range(4):
@@ -62,7 +64,7 @@ def tile_list_linen_wear_scores_kernel(
         def load_vec(dst, src):
             nc.sync.dma_start(out=dst[:], in_=src.rearrange("(b p t) -> p b t", b=PASS2, t=PACK))
 
-        tab_sb = [keep.tile([P, T], U32, name="tab%d" % a) for a in range(PASS1)]
+        tab_sb = [keep.tile([P, T], U32, name="tab%d" % a, align_bytes=64) for a in range(PASS1)]
         w4_raw = keep.tile([P, PASS2 * 2 * H], U8, name="w4_raw")
 
         def load_tab(a):
@@ -74,8 +76,8 @@ def tile_list_linen_wear_scores_kernel(
         def load_w1(a, c0, width):
             if width < KP:
                 raw = ring.tile([P, PACK, width], F32, name="w1_half")
-            elif c0 and a == PASS1 - 1:
-                raw = keep.tile([P, PACK, width], F32, name="raw_last")
+            elif c0 and a:
+                raw = keep.tile([P, PACK, width], F32, name="raw_late%d" % a)
             else:
                 raw = ring.tile([P, PACK, width], F32, name="w1_raw")
             nc.sync.dma_start(
@@ -90,8 +92,8 @@ def tile_list_linen_wear_scores_kernel(
         )
         nc.sync.dma_start(offs_sb[:], offs)
         raw = {}
-        raw[(0, 0)] = [load_w1(0, 0, KP)]
         load_tab(0)
+        raw[(0, 0)] = [load_w1(0, 0, KP)]
         raw[(0, 1)] = [load_w1(1, 0, KP)]
         for q in range(4):
             nc.sync.dma_start(
@@ -114,9 +116,9 @@ def tile_list_linen_wear_scores_kernel(
                 grouped = keep.tile([P, PACK * KP], BF16, name="w1_late%d" % a, align_bytes=64)
             else:
                 grouped = ring.tile([P, PACK * KP], BF16, name="w1_bf", align_bytes=64)
-            view = grouped[:].rearrange("p (t m j) -> p m t j", t=PACK, j=PACK)
+            view = grouped[:].rearrange("p (t m j) -> p m j t", t=PACK, j=PACK)
             pieces = raw[(b, a)]
-            srcs = [piece[:].rearrange("p j (m t) -> p m t j", t=PACK) for piece in pieces]
+            srcs = [piece[:].rearrange("p j (m t) -> p m j t", t=PACK) for piece in pieces]
             per = P // len(srcs)
             for n, src in enumerate(srcs):
                 dst = view[:, n * per : (n + 1) * per]
@@ -140,7 +142,6 @@ def tile_list_linen_wear_scores_kernel(
             w1_sc[(b, a)] = sc
 
         v_codes = [keep.tile([P, S], U32, name="v%d" % a, align_bytes=64) for a in range(PASS1)]
-        v_sc = keep.tile([P, S], U8, name="v_sc", align_bytes=64)
 
         def gather_tab(a):
             for half in range(S // BANK):
@@ -162,20 +163,28 @@ def tile_list_linen_wear_scores_kernel(
                 stop=(a == PASS1 - 1),
             )
 
-        feat = [keep.tile([P, S], F32, name="feat%d" % i) for i in range(TILES)]
+        feat = {}
 
         def silu(acc, b, t, half):
+            if half == 0:
+                i = PACK * b + t
+                name = "raw_late2" if i == PACK - 1 else "feat%d" % i
+                feat[i] = keep.tile([P, S], F32, name=name)
             nc.scalar.activation(
                 feat[PACK * b + t][:, half * BANK : (half + 1) * BANK], acc[:], ACT.Silu, bias=b1_sb[:, b, t : t + 1]
             )
 
         w4_sb = keep.tile([P, PASS2 * 2 * H], U8, name="w4_sb", align_bytes=64)
         w4_sc = keep.tile([P, PASS2 * H], U8, name="w4_sc", align_bytes=64)
+        gather_tab(0)
+        v_sc = keep.tile([P, S], U8, name="tab0", align_bytes=64)
         nc.vector.tensor_copy(v_sc[:], tab_sc[:].indirect(offs_sb[:]))
         for a in range(PASS1):
-            gather_tab(a)
+            if a:
+                gather_tab(a)
             grouped = cast_w1(0, a)
             quant_w1(0, a, grouped, PACK if a == PASS1 - 1 else 1)
+        held = []
         for a in range(PASS1):
             raw[(1, a)] = [load_w1(a, KP, KP)]
         load_vec(gs_sb, gs)
@@ -185,7 +194,10 @@ def tile_list_linen_wear_scores_kernel(
                 acc = psum.tile([P, BANK], F32, name="acc")
                 for a in range(PASS1):
                     mm1(acc, 0, t, a, half)
-                silu(acc, 0, t, half)
+                if t < PACK - 1:
+                    silu(acc, 0, t, half)
+                else:
+                    held.append(acc)
 
         for a in range(PASS2):
             cols = slice(a * 2 * H, (a + 1) * 2 * H)
@@ -201,6 +213,8 @@ def tile_list_linen_wear_scores_kernel(
         for a in range(PASS1):
             grouped = cast_w1(1, a)
             quant_w1(1, a, grouped, PACK if a == PASS1 - 1 else 1)
+        for half in range(2):
+            silu(held[half], 0, PACK - 1, half)
         for t in range(PACK):
             for half in range(2):
                 acc = psum.tile([P, BANK], F32, name="acc")
@@ -209,7 +223,7 @@ def tile_list_linen_wear_scores_kernel(
                 silu(acc, 1, t, half)
 
         late = keep.tile([P, 2 * M + TILES], F32, name="w1c12", align_bytes=64)
-        early = keep.tile([P, 2 * M], F32, name="raw_last")
+        early = keep.tile([P, 2 * M], F32, name="raw_late1")
         planes = [x[:, : 2 * M].bitcast(BF16).rearrange("p (t m) -> p t m", t=PACK) for x in (early, late)]
         both = late[:, 2 * M :]
         z_codes = [keep.tile([P, M], U32, name="zc%d" % b, align_bytes=64) for b in range(PASS2)]
@@ -217,22 +231,40 @@ def tile_list_linen_wear_scores_kernel(
         second = {}
 
         def pick_second(i):
-            second[i] = ring.tile([P, M], F32, name="second", bufs=3)
-            nc.vector.tensor_copy(second[i][:], feat[i][:].indirect(pos2_sb[:]))
+            if i == PACK - 2:
+                second[i] = keep.tile([P, M], F32, name="w1_late1", align_bytes=64)
+            else:
+                second[i] = ring.tile([P, M], F32, name="second")
+            for h in range(2):
+                nc.vector.tensor_copy(
+                    second[i][:, h * HALF : (h + 1) * HALF],
+                    feat[i][:].indirect(pos2_sb[:, h * (HALF // 16) : (h + 1) * (HALF // 16)]),
+                )
 
         def difference(i):
             b, t = divmod(i, PACK)
-            if i in (PACK - 2, PACK - 1):
-                diff = keep.tile([P, M], F32, name="w1_late%d" % (i - 1), align_bytes=64)
+            if i == PACK - 2:
+                diff = keep.tile([P, M], F32, name="w1_late2", align_bytes=64)
             elif i == TILES - 1:
                 diff = keep.tile([P, M], F32, name="b1_sb", align_bytes=64)
             else:
                 diff = ring.tile([P, M], F32, name="diff", bufs=4)
-            nc.vector.tensor_tensor(diff[:], feat[i][:].indirect(pos1_sb[:]), second[i][:], ALU.subtract)
+            for h in range(2):
+                cols = slice(h * HALF, (h + 1) * HALF)
+                nc.vector.tensor_tensor(
+                    diff[:, cols],
+                    feat[i][:].indirect(pos1_sb[:, h * (HALF // 16) : (h + 1) * (HALF // 16)]),
+                    second[i][:, cols],
+                    ALU.subtract,
+                )
             if i < TILES - 1:
                 nc.scalar.activation(planes[b][:, t, :], diff[:], ACT.Copy, scale=gain_sb[:, b, t : t + 1])
             else:
-                nc.vector.tensor_scalar(planes[b][:, t, :], diff[:], gain_sb[:, b, t : t + 1], None, ALU.mult)
+                for h in range(2):
+                    cols = slice(h * HALF, (h + 1) * HALF)
+                    nc.vector.tensor_scalar(
+                        planes[b][:, t, cols], diff[:, cols], gain_sb[:, b, t : t + 1], None, ALU.mult
+                    )
 
         def quant_z(b):
             if b == 0:
@@ -243,14 +275,21 @@ def tile_list_linen_wear_scores_kernel(
             src = planes[b].rearrange("p t (c i) -> p c t i", i=4)
             if b == 0:
                 nc.scalar.copy(out=dst, in_=src)
+                nc.vector.quantize_mx(out=z_codes[b][:].bitcast(FP8X4), scales=z_sc[b][:], in_=woven)
             else:
-                nc.vector.tensor_copy(out=dst, in_=src)
-            nc.vector.quantize_mx(out=z_codes[b][:].bitcast(FP8X4), scales=z_sc[b][:], in_=woven)
+                for h in range(2):
+                    quads = slice(h * HALF // 4, (h + 1) * HALF // 4)
+                    nc.vector.tensor_copy(out=dst[:, quads], in_=src[:, quads])
+                for h in range(2):
+                    cols = slice(h * HALF, (h + 1) * HALF)
+                    nc.vector.quantize_mx(
+                        out=z_codes[b][:, cols].bitcast(FP8X4),
+                        scales=z_sc[b][:, cols],
+                        in_=woven[:, PACK * h * HALF : PACK * (h + 1) * HALF],
+                    )
 
-        pick_second(0)
         for i in range(TILES):
-            if i + 1 < TILES:
-                pick_second(i + 1)
+            pick_second(i)
             difference(i)
             if i % PACK == PACK - 1:
                 quant_z(i // PACK)
@@ -272,16 +311,14 @@ def tile_list_linen_wear_scores_kernel(
                     start=(a == 0),
                     stop=(a == PASS2 - 1),
                 )
-            nc.scalar.activation(resp[i][:, :M], acc[:], ACT.Tanh, scale=-1.0)
-            for half in range(S // BANK):
-                cols = slice(half * BANK, (half + 1) * BANK)
-                own = ring.tile([P, BANK], F32, name="own", bufs=4)
-                nc.scalar.activation(own[:], feat[i][:, cols], ACT.Copy, scale=both[:, i : i + 1])
-                res = ring.tile([P, BANK], F32, name="res", bufs=4)
+            window = resp[i % WINDOWS]
+            nc.scalar.activation(window[:, :M], acc[:], ACT.Tanh, scale=-1.0)
+            own = ring.tile([P, S], F32, name="own")
+            nc.scalar.activation(own[:], feat[i][:], ACT.Copy, scale=both[:, i : i + 1])
+            res = ring.tile([P, S], F32, name="res", bufs=3)
+            cuts = (0, S) if i < TILES - 1 else (0, S // 2, 3 * S // 4, S)
+            for c0, c1 in zip(cuts[:-1], cuts[1:]):
                 nc.vector.tensor_tensor(
-                    res[:],
-                    resp[i][:].indirect(pos3_sb[:, half * (BANK // 16) : (half + 1) * (BANK // 16)]),
-                    own[:],
-                    ALU.add,
+                    res[:, c0:c1], window[:].indirect(pos3_sb[:, c0 // 16 : c1 // 16]), own[:, c0:c1], ALU.add
                 )
-                nc.sync.dma_start(out=out_rows[b, t][:, cols], in_=res[:])
+                nc.sync.dma_start(out=out_rows[b, t][:, c0:c1], in_=res[:, c0:c1])

from contextlib import ExitStack

import concourse.mybir as mybir

K, H, T, S, M = 1536, 1024, 4096, 1024, 512
FLOPS = 2 * K * H * S + 2 * H * H * M

F32 = mybir.dt.float32
BF16 = mybir.dt.bfloat16
I32 = mybir.dt.int32
U32 = mybir.dt.uint32
U16 = mybir.dt.uint16
U8 = mybir.dt.uint8
FP8X4 = mybir.dt.float8_e4m3fn_x4
FP4X4 = mybir.dt.float4_e2m1fn_x4
ACT = mybir.ActivationFunctionType
ALU = mybir.AluOpType

P = 128
PACK = 4
KP = P * PACK
BANK = 512
PASS1 = K // KP
PASS2 = H // KP
TILES = H // P
SPARE = 32
WINDOWS = 4
HALF = M // 2


def tile_list_linen_wear_scores_kernel(
    tc, tab_words, tab_scales, offs, pos1, pos2, pos3, w1, b1, gain, w4_words, w4_scales, gs, out
):
    nc = tc.nc
    with ExitStack() as ctx:
        keep = ctx.enter_context(tc.tile_pool(name="keep", bufs=1))
        ring = ctx.enter_context(tc.tile_pool(name="ring", bufs=2))
        psum = ctx.enter_context(tc.psum_pool(name="psum", bufs=8))

        offs_sb = keep.tile([P, S // 16], U16, name="offs_sb")
        pos1_sb = keep.tile([P, M // 16], U16, name="pos1_sb")
        pos2_sb = keep.tile([P, M // 16], U16, name="pos2_sb")
        pos3_sb = keep.tile([P, S // 16], U16, name="pos3_sb")

        tab_sc = keep.tile([P, T], U8, name="tab_sc", align_bytes=64)
        w4_sc_raw = keep.tile([P, PASS2 * H], U8, name="w4_sc_raw", align_bytes=64)
        zeros = keep.tile([P, S + SPARE - M], F32, name="zeros")
        nc.vector.memset(tab_sc[:].bitcast(I32), 0)
        nc.gpsimd.memset(w4_sc_raw[:].bitcast(I32), 0)
        nc.vector.memset(zeros[:], 0.0)
        resp = [keep.tile([P, S + SPARE], F32, name="resp%d" % i) for i in range(WINDOWS)]
        for i in range(WINDOWS):
            nc.scalar.activation(resp[i][:, M:], zeros[:], ACT.Silu)

        for q in range(4):
            nc.gpsimd.dma_start(
                out=tab_sc[32 * q : 32 * q + 4 * PASS1, :].bitcast(I32),
                in_=tab_scales[:, 4 * q : 4 * q + 4, :].bitcast(I32),
            )
        b1_sb = keep.tile([P, PASS2, PACK], F32, name="b1_sb", align_bytes=64)
        gain_sb = keep.tile([P, PASS2, PACK], F32, name="gain_sb")
        gs_sb = keep.tile([P, PASS2, PACK], F32, name="gs_sb")

        def load_vec(dst, src):
            nc.sync.dma_start(out=dst[:], in_=src.rearrange("(b p t) -> p b t", b=PASS2, t=PACK))

        tab_sb = [keep.tile([P, T], U32, name="tab%d" % a, align_bytes=64) for a in range(PASS1)]
        w4_raw = keep.tile([P, PASS2 * 2 * H], U8, name="w4_raw")

        def load_tab(a):
            nc.sync.dma_start(
                out=tab_sb[a][:].bitcast(I32),
                in_=tab_words[a].rearrange("p t i -> p (t i)").bitcast(I32),
            )

        def load_w1(a, c0, width):
            if width < KP:
                raw = ring.tile([P, PACK, width], F32, name="w1_half")
            elif c0 and a:
                raw = keep.tile([P, PACK, width], F32, name="raw_late%d" % a)
            else:
                raw = ring.tile([P, PACK, width], F32, name="w1_raw")
            nc.sync.dma_start(
                out=raw[:],
                in_=w1[a * KP : (a + 1) * KP, c0 : c0 + width].rearrange("(p j) c -> p j c", j=PACK),
            )
            return raw

        nc.sync.dma_start(
            out=w4_raw[:].bitcast(I32).rearrange("p (a n) -> p a n", a=PASS2),
            in_=w4_words.bitcast(I32).rearrange("a p n -> p a n"),
        )
        nc.sync.dma_start(offs_sb[:], offs)
        raw = {}
        load_tab(0)
        raw[(0, 0)] = [load_w1(0, 0, KP)]
        raw[(0, 1)] = [load_w1(1, 0, KP)]
        for q in range(4):
            nc.sync.dma_start(
                out=w4_sc_raw[32 * q : 32 * q + 4, :].bitcast(I32).rearrange("r (a n) -> r a n", a=PASS2),
                in_=w4_scales[:, 4 * q : 4 * q + 4, :].bitcast(I32).rearrange("a r n -> r a n"),
            )
        load_vec(b1_sb, b1)
        load_tab(1)
        nc.sync.dma_start(pos2_sb[:], pos2)
        load_tab(2)
        raw[(0, 2)] = [load_w1(2, 0, KP // 2), load_w1(2, KP // 2, KP // 2)]
        load_vec(gain_sb, gain)
        nc.sync.dma_start(pos1_sb[:], pos1)

        w1_codes = {}
        w1_sc = {}

        def cast_w1(b, a):
            if b == 1 and a > 0:
                grouped = keep.tile([P, PACK * KP], BF16, name="w1_late%d" % a, align_bytes=64)
            else:
                grouped = ring.tile([P, PACK * KP], BF16, name="w1_bf", align_bytes=64)
            view = grouped[:].rearrange("p (t m j) -> p m j t", t=PACK, j=PACK)
            pieces = raw[(b, a)]
            srcs = [piece[:].rearrange("p j (m t) -> p m j t", t=PACK) for piece in pieces]
            per = P // len(srcs)
            for n, src in enumerate(srcs):
                dst = view[:, n * per : (n + 1) * per]
                if n == 0 and (b, a) != (1, 0):
                    nc.scalar.copy(out=dst, in_=src)
                else:
                    nc.vector.tensor_copy(out=dst, in_=src)
            return grouped

        def quant_w1(b, a, grouped, parts):
            codes = keep.tile([P, KP], U32, name="w1c%d%d" % (b, a), align_bytes=64)
            sc = keep.tile([P, KP], U8, name="w1s%d%d" % (b, a), align_bytes=64)
            w = KP // parts
            for n in range(parts):
                nc.vector.quantize_mx(
                    out=codes[:, n * w : (n + 1) * w].bitcast(FP8X4),
                    scales=sc[:, n * w : (n + 1) * w],
                    in_=grouped[:, PACK * n * w : PACK * (n + 1) * w],
                )
            w1_codes[(b, a)] = codes
            w1_sc[(b, a)] = sc

        v_codes = [keep.tile([P, S], U32, name="v%d" % a, align_bytes=64) for a in range(PASS1)]

        def gather_tab(a):
            for half in range(S // BANK):
                nc.vector.tensor_copy(
                    v_codes[a][:, half * BANK : (half + 1) * BANK],
                    tab_sb[a][:].indirect(offs_sb[:, half * (BANK // 16) : (half + 1) * (BANK // 16)]),
                )

        def mm1(acc, b, t, a, half):
            cols = slice(half * BANK, (half + 1) * BANK)
            rows = slice(t * P, (t + 1) * P)
            nc.tensor.matmul_mx(
                out=acc[:],
                lhsT=w1_codes[(b, a)][:, rows].bitcast(FP8X4),
                lhsT_scale=w1_sc[(b, a)][:, rows],
                rhs=v_codes[a][:, cols].bitcast(FP8X4),
                rhs_scale=v_sc[4 * a : P, cols],
                start=(a == 0),
                stop=(a == PASS1 - 1),
            )

        feat = {}

        def silu(acc, b, t, half):
            if half == 0:
                i = PACK * b + t
                name = "raw_late2" if i == PACK - 1 else "feat%d" % i
                feat[i] = keep.tile([P, S], F32, name=name)
            nc.scalar.activation(
                feat[PACK * b + t][:, half * BANK : (half + 1) * BANK], acc[:], ACT.Silu, bias=b1_sb[:, b, t : t + 1]
            )

        w4_sb = keep.tile([P, PASS2 * 2 * H], U8, name="w4_sb", align_bytes=64)
        w4_sc = keep.tile([P, PASS2 * H], U8, name="w4_sc", align_bytes=64)
        gather_tab(0)
        v_sc = keep.tile([P, S], U8, name="tab0", align_bytes=64)
        nc.vector.tensor_copy(v_sc[:], tab_sc[:].indirect(offs_sb[:]))
        for a in range(PASS1):
            if a:
                gather_tab(a)
            grouped = cast_w1(0, a)
            quant_w1(0, a, grouped, PACK if a == PASS1 - 1 else 1)
        held = []
        for a in range(PASS1):
            raw[(1, a)] = [load_w1(a, KP, KP)]
        load_vec(gs_sb, gs)
        nc.sync.dma_start(pos3_sb[:], pos3)
        for t in range(PACK):
            for half in range(2):
                acc = psum.tile([P, BANK], F32, name="acc")
                for a in range(PASS1):
                    mm1(acc, 0, t, a, half)
                if t < PACK - 1:
                    silu(acc, 0, t, half)
                else:
                    held.append(acc)

        for a in range(PASS2):
            cols = slice(a * 2 * H, (a + 1) * 2 * H)
            nc.vector.tensor_copy(
                out=w4_sb[:, cols].rearrange("p (b t q e) -> p b t q e", b=PASS2, t=PACK, e=2),
                in_=w4_raw[:, cols].rearrange("p (b q t e) -> p b t q e", b=PASS2, t=PACK, e=2),
            )
        nc.vector.tensor_copy(
            out=w4_sc[:].rearrange("p (g t q) -> p g t q", t=PACK, q=P),
            in_=w4_sc_raw[:].rearrange("p (g q t) -> p g t q", t=PACK, q=P),
        )

        for a in range(PASS1):
            grouped = cast_w1(1, a)
            quant_w1(1, a, grouped, PACK if a == PASS1 - 1 else 1)
        for half in range(2):
            silu(held[half], 0, PACK - 1, half)
        for t in range(PACK):
            for half in range(2):
                acc = psum.tile([P, BANK], F32, name="acc")
                for a in range(PASS1):
                    mm1(acc, 1, t, a, half)
                silu(acc, 1, t, half)

        late = keep.tile([P, 2 * M + TILES], F32, name="w1c12", align_bytes=64)
        early = keep.tile([P, 2 * M], F32, name="raw_late1")
        planes = [x[:, : 2 * M].bitcast(BF16).rearrange("p (t m) -> p t m", t=PACK) for x in (early, late)]
        both = late[:, 2 * M :]
        z_codes = [keep.tile([P, M], U32, name="zc%d" % b, align_bytes=64) for b in range(PASS2)]
        z_sc = [keep.tile([P, M], U8, name="zs%d" % b, align_bytes=64) for b in range(PASS2)]
        second = {}

        def pick_second(i):
            if i == PACK - 2:
                second[i] = keep.tile([P, M], F32, name="w1_late1", align_bytes=64)
            else:
                second[i] = ring.tile([P, M], F32, name="second")
            for h in range(2):
                nc.vector.tensor_copy(
                    second[i][:, h * HALF : (h + 1) * HALF],
                    feat[i][:].indirect(pos2_sb[:, h * (HALF // 16) : (h + 1) * (HALF // 16)]),
                )

        def difference(i):
            b, t = divmod(i, PACK)
            if i == PACK - 2:
                diff = keep.tile([P, M], F32, name="w1_late2", align_bytes=64)
            elif i == TILES - 1:
                diff = keep.tile([P, M], F32, name="b1_sb", align_bytes=64)
            else:
                diff = ring.tile([P, M], F32, name="diff", bufs=4)
            for h in range(2):
                cols = slice(h * HALF, (h + 1) * HALF)
                nc.vector.tensor_tensor(
                    diff[:, cols],
                    feat[i][:].indirect(pos1_sb[:, h * (HALF // 16) : (h + 1) * (HALF // 16)]),
                    second[i][:, cols],
                    ALU.subtract,
                )
            if i < TILES - 1:
                nc.scalar.activation(planes[b][:, t, :], diff[:], ACT.Copy, scale=gain_sb[:, b, t : t + 1])
            else:
                for h in range(2):
                    cols = slice(h * HALF, (h + 1) * HALF)
                    nc.vector.tensor_scalar(
                        planes[b][:, t, cols], diff[:, cols], gain_sb[:, b, t : t + 1], None, ALU.mult
                    )

        def quant_z(b):
            if b == 0:
                woven = keep.tile([P, M * PACK], BF16, name="b1_sb", align_bytes=64)[:]
            else:
                woven = ring.tile([P, M * PACK], BF16, name="w1_bf", align_bytes=64)[:]
            dst = woven.rearrange("p (c i t) -> p c t i", i=4, t=PACK)
            src = planes[b].rearrange("p t (c i) -> p c t i", i=4)
            if b == 0:
                nc.scalar.copy(out=dst, in_=src)
                nc.vector.quantize_mx(out=z_codes[b][:].bitcast(FP8X4), scales=z_sc[b][:], in_=woven)
            else:
                for h in range(2):
                    quads = slice(h * HALF // 4, (h + 1) * HALF // 4)
                    nc.vector.tensor_copy(out=dst[:, quads], in_=src[:, quads])
                for h in range(2):
                    cols = slice(h * HALF, (h + 1) * HALF)
                    nc.vector.quantize_mx(
                        out=z_codes[b][:, cols].bitcast(FP8X4),
                        scales=z_sc[b][:, cols],
                        in_=woven[:, PACK * h * HALF : PACK * (h + 1) * HALF],
                    )

        for i in range(TILES):
            pick_second(i)
            difference(i)
            if i % PACK == PACK - 1:
                quant_z(i // PACK)

        nc.vector.tensor_tensor(
            both, gs_sb[:].rearrange("p b t -> p (b t)"), gain_sb[:].rearrange("p b t -> p (b t)"), ALU.mult
        )
        out_rows = out.rearrange("(b p t) j -> b t p j", b=PASS2, t=PACK)
        for i in range(TILES):
            b, t = divmod(i, PACK)
            acc = psum.tile([P, BANK], F32, name="acc")
            for a in range(PASS2):
                nc.tensor.matmul_mx(
                    out=acc[:],
                    lhsT=w4_sb[:, a * 2 * H + i * 2 * P : a * 2 * H + (i + 1) * 2 * P].bitcast(FP4X4),
                    lhsT_scale=w4_sc[:, a * H + i * P : a * H + (i + 1) * P],
                    rhs=z_codes[a][:].bitcast(FP8X4),
                    rhs_scale=z_sc[a][:],
                    start=(a == 0),
                    stop=(a == PASS2 - 1),
                )
            window = resp[i % WINDOWS]
            nc.scalar.activation(window[:, :M], acc[:], ACT.Tanh, scale=-1.0)
            own = ring.tile([P, S], F32, name="own")
            nc.scalar.activation(own[:], feat[i][:], ACT.Copy, scale=both[:, i : i + 1])
            res = ring.tile([P, S], F32, name="res", bufs=3)
            cuts = (0, S) if i < TILES - 1 else (0, S // 2, 3 * S // 4, S)
            for c0, c1 in zip(cuts[:-1], cuts[1:]):
                nc.vector.tensor_tensor(
                    res[:, c0:c1], window[:].indirect(pos3_sb[:, c0 // 16 : c1 // 16]), own[:, c0:c1], ALU.add
                )
                nc.sync.dma_start(out=out_rows[b, t][:, c0:c1], in_=res[:, c0:c1])
